import numpy as np
import ml_dtypes


def mxq(x, axis, fmt="e4m3"):
    dtype, down = {"e4m3": (ml_dtypes.float8_e4m3fn, 7), "e5m2": (ml_dtypes.float8_e5m2, 14)}[fmt]
    v = np.moveaxis(np.asarray(x, np.float32).astype(ml_dtypes.bfloat16).astype(np.float64), axis, -1)
    blocks = v.reshape(v.shape[:-1] + (-1, 32))
    amax = np.abs(blocks).max(-1, keepdims=True)
    byte = np.maximum(np.where(amax > 0, np.frexp(amax)[1] - 1 + 127, 0) - down, 1)
    scale = np.exp2(byte - 127.0)
    codes = (blocks / scale).astype(np.float32).astype(dtype).astype(np.float64)
    return np.moveaxis((codes * scale).reshape(v.shape), -1, axis)


WIDE = False


def mx_kscale(k):
    if not WIDE:
        return np.ones(k)
    levels = np.array([10, -10, 5, -5, 0])
    if k % 512:
        return np.exp2(np.random.permutation(np.resize(levels, k // 32))).repeat(32)
    a = np.empty((k // 512, 16))
    for p in range(k // 512):
        a[p, :8] = np.random.permutation(np.resize(levels, 8))
        for g in range(8):
            far = levels[np.abs(levels - a[p, g]) >= 10]
            a[p, g + 8] = far[np.random.randint(len(far))]
    return np.exp2(a.ravel()).repeat(32)


BF16 = ml_dtypes.bfloat16


def bf(x):
    return np.asarray(x, np.float32).astype(BF16)


def f64(x):
    return np.asarray(x).astype(np.float64)


E2M1 = np.array([0.0, 0.5, 1.0, 1.5, 2.0, 3.0, 4.0, 6.0, -0.0, -0.5, -1.0, -1.5, -2.0, -3.0, -4.0, -6.0])


def pack_weight(w, fmt):
    k, n = w.shape
    w = f64(bf(w)).reshape(k // 32, 32, n)
    amax = np.abs(w).max(1)
    if fmt == "e4m3":
        byte = np.frexp(amax)[1] - 1 + 127 - 7
    else:
        mant, ex = np.frexp(amax / 6.0)
        byte = np.where(mant > 0.5, ex, ex - 1) + 127
    byte = np.clip(np.where(amax > 0, byte, 1), 1, 254)
    scaled = (w * np.exp2(127.0 - byte)[:, None, :]).reshape(k, n).astype(np.float32)
    by_word = np.ascontiguousarray(scaled.reshape(k // 512, 128, 4, n).transpose(0, 1, 3, 2))
    if fmt == "e4m3":
        words = by_word.astype(ml_dtypes.float8_e4m3fn).view(np.uint8)
    else:
        c = by_word.astype(ml_dtypes.float4_e2m1fn).view(np.uint8) & 0xF
        words = c[..., 0::2] | (c[..., 1::2] << 4)
    return np.ascontiguousarray(words), np.ascontiguousarray(byte.astype(np.uint8).reshape(k // 512, 16, n))


def unpack_weight(words, scales, fmt):
    g, p, n, _ = words.shape
    if fmt == "e4m3":
        vals = np.ascontiguousarray(words).view(ml_dtypes.float8_e4m3fn).astype(np.float64)
    else:
        nib = np.empty((g, p, n, 4), np.uint8)
        nib[..., 0::2] = words & 0xF
        nib[..., 1::2] = words >> 4
        vals = E2M1[nib]
    vals = vals * np.repeat(np.exp2(scales.astype(np.float64) - 127.0), 8, axis=1)[..., None]
    return vals.transpose(0, 1, 3, 2).reshape(g * 512, n)
def pack4(w):
    words, scales = pack_weight(w, "e2m1")
    return words.reshape(words.shape[0], 128, -1), scales


def unpack4(words, scales):
    return unpack_weight(words.reshape(words.shape[0], 128, -1, 2), scales, "e2m1")


E4M3FN = np.array([(-1.0 if i & 128 else 1.0) * ((1.0 + (i & 7) / 8.0) * 2.0 ** (((i >> 3) & 15) - 7) if i & 120 else (i & 7) * 2.0 ** -9) for i in range(256)])


def e4m3fn_bytes(y):
    return np.clip(np.asarray(y, np.float64), -448.0, 448.0).astype(np.float32).astype(ml_dtypes.float8_e4m3fn).view(np.uint8)


def e4m3fn_values(b):
    return E4M3FN[b]


T, K, F, R, B = 1024, 2048, 1024, 512, 128


def setup_inputs():
    s, t = mx_kscale(K), mx_kscale(F)
    x = np.random.standard_normal((T, K)) * s
    x_scale = (np.abs(x).reshape(T, K // B, B).max(axis=2) / 448.0).astype(np.float32)
    x_bytes = e4m3fn_bytes(x / np.repeat(f64(x_scale), B, axis=1))
    w = bf(np.random.standard_normal((K, F)) / np.sqrt(K) / s[:, None] * t)
    b = bf(0.4 * np.random.standard_normal(F) * t)
    v_words, v_scales = pack4(np.random.standard_normal((F, R)) / np.sqrt(F) / t[:, None])
    shift = bf(0.4 * np.random.standard_normal(R))
    return {"x_bytes": x_bytes, "x_scale": x_scale, "w": w, "b": b,
            "v_words": v_words, "v_scales": v_scales, "shift": shift}


def reference(x_bytes, x_scale, w, b, v_words, v_scales, shift):
    x = e4m3fn_values(x_bytes) * np.repeat(f64(x_scale), B, axis=1)
    y = mxq(x, 1, "e4m3") @ mxq(f64(w), 0, "e4m3")
    h = np.maximum(y + f64(b), 0.0)
    score = mxq(h, 1, "e4m3") @ unpack4(v_words, v_scales)
    return score - f64(shift)

from contextlib import ExitStack

import concourse.mybir as mybir
from concourse.masks import make_identity

T, K, F, R, B = 1024, 2048, 1024, 512, 128
FLOPS = 2 * T * K * F + 2 * T * F * R

F32 = mybir.dt.float32
BF16 = mybir.dt.bfloat16
U32 = mybir.dt.uint32
I32 = mybir.dt.int32
U8 = mybir.dt.uint8
F8 = mybir.dt.float8_e4m3fn
F8X4 = mybir.dt.float8_e4m3fn_x4
F4X4 = mybir.dt.float4_e2m1fn_x4
ACT = mybir.ActivationFunctionType
ALU = mybir.AluOpType

SIZES = [1,2,2,2,1]
START = [sum(SIZES[:c]) for c in range(len(SIZES))]
CHUNK = [c for c, n in enumerate(SIZES) for i in range(n)]
LOADS = "x0 w00 x1 w01 w02 w03 x2 x3 w10 w11 w12 w13 x4 x5 x6 x7"
ORDER = """
A01V D00V A00S T01P B01S T00P C01V D01S W0P W1P A10S W2P A11V T11P B00S E00V
W3P T10P D02V E01V A21S A20V E02V B11S T20P T21P D03V C00V B10S E03V A31S B20S
D10V M001P B21S D13V A30S M000P C11V T31P M003P C10V A41S B31S M002P A40V D12V M102P
D11S F003S E10V M103P M101P T41P E12V F000S T30P F002S E13V F001S F102S F103S T40P E11V
M100P M112P M010P M113P M011P F101S F100V M110P A50V B40S B41S B30S F112S F113S A70V F110S
M013P A60V C20V C21V M012P I00S F012V M111P F013S A61V F010S T50P T70P T60P M210P A51V
I10V F111S A71V F011S B50S B70S B60S M211P M203P M202P F210S T61P T51P Q10V F211S I11V
F203S B61V T71P I01S C30V B51S C31V F202S C40V N100P B71S M212P Q11V N110P M213P F213S
M201P M200P F212S F201S M303P N111P F200S M310P C41V N101P M302P M301P I21S Q01V M300P I20V
F302S F303V M311P F310S F300S Q20V Q21V H10V N200P M312P N201P F301V F311S M401P M403P F312S
Q00V H11V M313P M400P I30V M412P F403S F401S N210P Q30V F313S F400S H20V I31V N211P M411P
H21V F412S M402P F402S N000P N001P M413P Q31V F411V M410P H00V N300P I40S N301P F413S N310P
N311P F410S Q40V I41S H30V N400P Q41V H31V N401P H40V
"""


def tile_reward_head_score_d4_kernel(tc, x_bytes, x_scale, w, b, v_words, v_scales, shift, out):
    nc = tc.nc
    xv = x_bytes.rearrange("(p a) k -> p a k", a=8)
    ov = out.rearrange("(p a) r -> p a r", a=8)
    with ExitStack() as ctx:
        keep = ctx.enter_context(tc.tile_pool(name="keep", bufs=1))
        psum = ctx.enter_context(tc.psum_pool(name="psum", bufs=1))
        ctx.enter_context(tc.manual_schedule())

        xs = keep.tile([128, 128], F32, name="xs")
        nc.scalar.dma_start(out=xs[:], in_=x_scale.rearrange("(p a) j -> p (a j)", a=8))
        bb = keep.tile([128, 2, 4], BF16, name="bb")
        nc.scalar.dma_start(out=bb[:], in_=b.rearrange("(g p t) -> p g t", p=128, t=4))
        ident = keep.tile([128, 128], F32, name="ident")
        make_identity(nc, ident[:])
        vs = keep.tile([128, 2, 512], U8, name="vs", align_bytes=64)
        nc.gpsimd.memset(vs[:].rearrange("p g n -> p (g n)").bitcast(I32), 0)
        bf = keep.tile([128, 8], F32, name="bf")
        nc.gpsimd.tensor_copy(out=bf[:], in_=bb[:].rearrange("p g t -> p (g t)"))

        xb = {}
        wr = {}
        for item in LOADS.split():
            if item[0] == "x":
                t = int(item[1])
                xb[t] = keep.tile([128, 2048], U8, name="xb" + item, align_bytes=64)
                parts = 2 if t == 0 else 1
                for i in range(parts):
                    cols = slice(2048 // parts * i, 2048 // parts * (i + 1))
                    nc.sync.dma_start(out=xb[t][:, cols], in_=xv[:, t, cols])
            else:
                gf, g = int(item[1]), int(item[2])
                wr[gf, g] = keep.tile([128, 4, 512], BF16, name="wr" + item, align_bytes=64)
                nc.sync.dma_start(
                    out=wr[gf, g][:],
                    in_=w[512 * g : 512 * (g + 1), 512 * gf : 512 * (gf + 1)].rearrange("(p j) f -> p j f", j=4),
                )
        vw = keep.tile([128, 2, 1024], U8, name="vw", align_bytes=64)
        nc.sync.dma_start(out=vw[:].bitcast(I32), in_=v_words.rearrange("g p c -> p g c").bitcast(I32))
        for q in range(4):
            nc.sync.dma_start(
                out=vs[32 * q : 32 * q + 4, :, :].bitcast(I32),
                in_=v_scales[:, 4 * q : 4 * q + 4, :].rearrange("g q n -> q g n").bitcast(I32),
            )
        sh = keep.tile([128, 512], BF16, name="sh")
        nc.sync.dma_start(out=sh[:], in_=shift.partition_broadcast(128))

        xw, xg, xc, xcs = {}, {}, {}, {}
        wg, wc, wcs = {}, {}, {}
        hp, hg, hc, hcs = {}, {}, {}, {}
        tp, m1, m2 = {}, {}, {}
        packed = {}

        def A(t, h, e):
            if t not in xw:
                xw[t] = keep.tile([128, 2048], BF16, name="xw%d" % t, align_bytes=64)
            packed[t, h] = e == "V" and True
            for j in range(8 * h, 8 * h + 8):
                g, q = j // 4, j % 4
                src = xb[t][:, 128 * j : 128 * (j + 1)].bitcast(F8)
                dst = xw[t][:, 128 * j : 128 * (j + 1)]
                s = xs[:, 16 * t + j : 16 * t + j + 1]
                if e == "S":
                    nc.scalar.activation(out=dst, in_=src, func=ACT.Copy, scale=s)
                elif not packed[t, h]:
                    nc.vector.tensor_scalar(out=dst, in0=src, scalar1=s, scalar2=None, op0=ALU.mult)
                else:
                    dst = xw[t][:, 512 * g : 512 * (g + 1)].rearrange("p (u w e) -> p w u e", u=2, e=2)[:, 32 * q : 32 * q + 32]
                    nc.vector.tensor_scalar(
                        out=dst, in0=src.rearrange("p (w u e) -> p w u e", u=2, e=2), scalar1=s, scalar2=None, op0=ALU.mult
                    )

        def TR(t, h):
            tp[t, h] = psum.tile([128, 2, 2, 128], F32, name="tp", bufs=3)
            words = xw[t][:].bitcast(F32)
            for i in range(2):
                g = 2 * h + i
                for u in range(2):
                    if packed[t, h]:
                        src = words[:, 256 * g + 128 * u : 256 * g + 128 * (u + 1)]
                    else:
                        src = words[:, 256 * g + u : 256 * (g + 1) : 2]
                    nc.tensor.transpose(tp[t, h][:, i, u, :], src, ident[:])

        def BC(t, h, e):
            c = CHUNK[t]
            k = t - START[c]
            if c not in xg:
                xg[c] = keep.tile([128, 2048 * SIZES[c]], BF16, name="xg%d" % c, align_bytes=64)
            dst = xg[c][:].bitcast(F32).rearrange("p (g r u) -> p g r u", g=4, u=2)
            dst = dst[:, 2 * h : 2 * h + 2, 128 * k : 128 * (k + 1), :]
            src = tp[t, h][:].rearrange("p g u r -> p g r u")
            if e == "S":
                nc.scalar.copy(out=dst, in_=src)
            else:
                nc.vector.tensor_copy(out=dst, in_=src)

        def C(c, h):
            if c not in xc:
                n = 512 * SIZES[c]
                xc[c] = keep.tile([128, n], U32, name="xc%d" % c, align_bytes=64)
                xcs[c] = keep.tile([128, n], U8, name="xcs%d" % c, align_bytes=64)
            half = 256 * SIZES[c]
            cols = slice(half * h, half * (h + 1))
            nc.vector.quantize_mx(
                out=xc[c][:, cols].bitcast(F8X4), scales=xcs[c][:, cols], in_=xg[c][:, 4 * half * h : 4 * half * (h + 1)]
            )

        def D(gf, g, e):
            wg[gf, g] = keep.tile([128, 2048], BF16, name="wg", bufs=5, align_bytes=64)
            dst = wg[gf, g][:].rearrange("p (t n i j) -> p n t i j", t=4, i=2, j=4)
            src = wr[gf, g][:].rearrange("p j (n i t) -> p n t i j", i=2, t=4)
            if e == "S":
                nc.scalar.copy(out=dst, in_=src)
            else:
                nc.vector.tensor_copy(out=dst, in_=src)

        def E(gf, g):
            wc[gf, g] = keep.tile([128, 512], U32, name="wc%d%d" % (gf, g), align_bytes=64)
            wcs[gf, g] = keep.tile([128, 512], U8, name="wcs%d%d" % (gf, g), align_bytes=64)
            nc.vector.quantize_mx(out=wc[gf, g][:].bitcast(F8X4), scales=wcs[gf, g][:], in_=wg[gf, g][:])

        def mm1(dst, c, gf, t, g):
            wide = 128 * SIZES[c]
            nc.tensor.matmul_mx(
                out=dst,
                lhsT=wc[gf, g][:, 128 * t : 128 * (t + 1)].bitcast(F8X4),
                lhsT_scale=wcs[gf, g][:, 128 * t : 128 * (t + 1)],
                rhs=xc[c][:, wide * g : wide * (g + 1)].bitcast(F8X4),
                rhs_scale=xcs[c][:, wide * g : wide * (g + 1)],
                start=(g == 0),
                stop=(g == 3),
            )

        def M1(c, gf, t):
            wide = 128 * SIZES[c]
            per = 4 // SIZES[c]
            if (c, gf) == (0, 0) and False:
                if t == 0:
                    for i in range(4):
                        bank = psum.tile([128, per, wide], F32, name="m1", bufs=3)
                        m1[c, gf, i] = bank[:, 0, :]
                for i in range(4):
                    mm1(m1[c, gf, i], c, gf, i, t)
                return
            if (c, gf, t) not in m1:
                bank = psum.tile([128, per, wide], F32, name="m1", bufs=3)
                for i in range(per):
                    m1[c, gf, t // per * per + i] = bank[:, i, :]
            for g in range(4):
                mm1(m1[c, gf, t], c, gf, t, g)

        def FC(c, gf, t, e):
            if (c, gf) not in hp:
                hp[c, gf] = keep.tile([128, 4, 128 * SIZES[c]], BF16, name="hp%d%d" % (c, gf), align_bytes=64)
            dst = hp[c, gf][:, t, :]
            bias = bf[:, 4 * gf + t : 4 * gf + t + 1]
            if e == "S":
                nc.scalar.activation(out=dst, in_=m1[c, gf, t], func=ACT.Relu, bias=bias)
            else:
                nc.vector.tensor_scalar(out=dst, in0=m1[c, gf, t], scalar1=bias, scalar2=0.0, op0=ALU.add, op1=ALU.max)

        def I(c, gf, e):
            hg[c, gf] = keep.tile([128, 512 * SIZES[c]], BF16, name="hg%d%d" % (c, gf), align_bytes=64)
            dst = hg[c, gf][:].rearrange("p (n i t) -> p n t i", i=4, t=4)
            src = hp[c, gf][:].rearrange("p t (n i) -> p n t i", i=4)
            if e == "S":
                nc.scalar.copy(out=dst, in_=src)
            else:
                nc.vector.tensor_copy(out=dst, in_=src)

        def Q(c, gf):
            hc[c, gf] = keep.tile([128, 128 * SIZES[c]], U32, name="hc%d%d" % (c, gf), align_bytes=64)
            hcs[c, gf] = keep.tile([128, 128 * SIZES[c]], U8, name="hcs%d%d" % (c, gf), align_bytes=64)
            nc.vector.quantize_mx(out=hc[c, gf][:].bitcast(F8X4), scales=hcs[c, gf][:], in_=hg[c, gf][:])

        def M2(c, k, gf):
            if gf == 0:
                m2[c, k] = psum.tile([128, 512], F32, name="m2", bufs=2)
            nc.tensor.matmul_mx(
                out=m2[c, k][:],
                lhsT=hc[c, gf][:, 128 * k : 128 * (k + 1)].bitcast(F8X4),
                lhsT_scale=hcs[c, gf][:, 128 * k : 128 * (k + 1)],
                rhs=vw[:, gf, :].bitcast(F4X4),
                rhs_scale=vs[:, gf, :],
                start=(gf == 0),
                stop=(gf == 1),
            )

        def WARM(i):
            if "w" not in m2:
                m2["w"] = psum.tile([128, 512], F32, name="m2", bufs=2)
            nc.tensor.matmul(m2["w"][:], lhsT=xw[0][:, 0:128], rhs=xw[0][:, 0:512], start=True, stop=True)

        def H(c, k):
            res = keep.tile([128, 512], F32, name="res", bufs=4)
            parts = 2 if START[c] + k == 7 else 1
            for i in range(parts):
                cols = slice(512 // parts * i, 512 // parts * (i + 1))
                nc.vector.tensor_tensor(out=res[:, cols], in0=m2[c, k][:, cols], in1=sh[:, cols], op=ALU.subtract)
                nc.sync.dma_start(out=ov[:, START[c] + k, cols], in_=res[:, cols])

        for item in ORDER.split():
            kind, e = item[0], item[-1]
            n = [int(ch) for ch in item[1:-1]]
            if kind == "A":
                A(n[0], n[1], e)
            elif kind == "T":
                TR(n[0], n[1])
            elif kind == "B":
                BC(n[0], n[1], e)
            elif kind == "C":
                C(n[0], n[1])
            elif kind == "D":
                D(n[0], n[1], e)
            elif kind == "E":
                E(n[0], n[1])
            elif kind == "M":
                M1(n[0], n[1], n[2])
            elif kind == "F":
                FC(n[0], n[1], n[2], e)
            elif kind == "I":
                I(n[0], n[1], e)
            elif kind == "Q":
                Q(n[0], n[1])
            elif kind == "N":
                M2(n[0], n[1], n[2])
            elif kind == "W":
                WARM(n[0])
            elif kind == "H":
                H(n[0], n[1])
